import numpy as np
import ml_dtypes


def mxq(x, axis, fmt="e4m3"):
    dtype, down = {"e4m3": (ml_dtypes.float8_e4m3fn, 7), "e5m2": (ml_dtypes.float8_e5m2, 14)}[fmt]
    v = np.moveaxis(np.asarray(x, np.float32).astype(ml_dtypes.bfloat16).astype(np.float64), axis, -1)
    blocks = v.reshape(v.shape[:-1] + (-1, 32))
    amax = np.abs(blocks).max(-1, keepdims=True)
    byte = np.maximum(np.where(amax > 0, np.frexp(amax)[1] - 1 + 127, 0) - down, 1)
    scale = np.exp2(byte - 127.0)
    codes = (blocks / scale).astype(np.float32).astype(dtype).astype(np.float64)
    return np.moveaxis((codes * scale).reshape(v.shape), -1, axis)


WIDE = False


def mx_kscale(k):
    if not WIDE:
        return np.ones(k)
    levels = np.array([10, -10, 5, -5, 0])
    if k % 512:
        return np.exp2(np.random.permutation(np.resize(levels, k // 32))).repeat(32)
    a = np.empty((k // 512, 16))
    for p in range(k // 512):
        a[p, :8] = np.random.permutation(np.resize(levels, 8))
        for g in range(8):
            far = levels[np.abs(levels - a[p, g]) >= 10]
            a[p, g + 8] = far[np.random.randint(len(far))]
    return np.exp2(a.ravel()).repeat(32)


def f64(x):
    return np.asarray(x).astype(np.float64)


def striped(idx):
    return np.tile(np.asarray(idx).reshape(-1, 16).T, (8, 1)).astype(np.uint16)


def unstriped(offs):
    return offs[:16].T.reshape(-1).astype(np.int64)


E2M1 = np.array([0.0, 0.5, 1.0, 1.5, 2.0, 3.0, 4.0, 6.0, -0.0, -0.5, -1.0, -1.5, -2.0, -3.0, -4.0, -6.0])


def pack_weight(w, fmt):
    k, n = w.shape
    w = f64(np.asarray(w, np.float32).astype(ml_dtypes.bfloat16)).reshape(k // 32, 32, n)
    amax = np.abs(w).max(1)
    if fmt == "e4m3":
        byte = np.frexp(amax)[1] - 1 + 127 - 7
    else:
        mant, ex = np.frexp(amax / 6.0)
        byte = np.where(mant > 0.5, ex, ex - 1) + 127
    byte = np.clip(np.where(amax > 0, byte, 1), 1, 254)
    scaled = (w * np.exp2(127.0 - byte)[:, None, :]).reshape(k, n).astype(np.float32)
    by_word = np.ascontiguousarray(scaled.reshape(k // 512, 128, 4, n).transpose(0, 1, 3, 2))
    if fmt == "e4m3":
        words = by_word.astype(ml_dtypes.float8_e4m3fn).view(np.uint8)
    else:
        c = by_word.astype(ml_dtypes.float4_e2m1fn).view(np.uint8) & 0xF
        words = (c[..., 0::2] | (c[..., 1::2] << 4)).reshape(k // 512, 128, 2 * n)
    return np.ascontiguousarray(words), np.ascontiguousarray(byte.astype(np.uint8).reshape(k // 512, 16, n))


def unpack_weight(words, scales, fmt):
    g, _, n = scales.shape
    words = np.ascontiguousarray(words).reshape(g, 128, n, -1)
    if fmt == "e4m3":
        vals = words.view(ml_dtypes.float8_e4m3fn).astype(np.float64)
    else:
        nib = np.empty((g, 128, n, 4), np.uint8)
        nib[..., 0::2] = words & 0xF
        nib[..., 1::2] = words >> 4
        vals = E2M1[nib]
    vals = vals * np.repeat(np.exp2(scales.astype(np.float64) - 127.0), 8, axis=1)[..., None]
    return vals.transpose(0, 1, 3, 2).reshape(g * 512, n)


def bf(x):
    return np.asarray(x, np.float32).astype(ml_dtypes.bfloat16)


def planes(Y):
    r, m = Y.shape
    b = f64(bf(Y)).reshape(r // 32, 32, m)
    amax = np.abs(b).max(1)
    byte = np.clip(np.where(amax > 0, np.frexp(amax)[1] - 1 + 127 - 7, 1), 1, 254)
    codes = (b * np.exp2(127.0 - byte)[:, None, :]).reshape(r, m).astype(np.float32).astype(ml_dtypes.float8_e4m3fn).view(np.uint8)
    words = codes.reshape(r // 512, 128, 4, m).transpose(0, 1, 3, 2)
    return np.ascontiguousarray(words), np.ascontiguousarray(byte.astype(np.uint8).reshape(r // 512, 16, m))


D, T, I, Q, E, J, C = 512, 2048, 512, 256, 512, 512, 1024


def setup_inputs():
    n = np.random.standard_normal
    idx = np.random.permutation(T)[:I]
    fd = mx_kscale(D)
    fc = mx_kscale(C)
    keysp = pack_weight(n((D, T)) / fd[:, None], "e2m1")
    return {
        "query": (n((D, Q)) * 0.4 / np.sqrt(D) * fd[:, None]).astype(np.float32),
        "keys_words": keysp[0],
        "keys_scales": keysp[1],
        "dkey": (n((D, J)) / fd[:, None]).astype(np.float32),
        "mask": (np.where(np.random.uniform(size=(Q, J)) < 0.3, 0.0, -30.0)).astype(np.float32),
        "fac": (np.random.uniform(0.5, 2.0, (1, C)) * fc).astype(np.float32),
        "vals": (n((C, E)) / fc[:, None]).astype(np.float32),
        "offs": striped(idx),
    }


def reference(query, keys_words, keys_scales, dkey, mask, fac, vals, offs):
    idx = unstriped(offs)
    keysu = unpack_weight(keys_words, keys_scales, "e2m1")
    queryq = mxq(f64(query), 0, "e4m3")
    keysidxg = keysu[:, idx]
    a = queryq.T @ keysidxg
    dkeyq = mxq(f64(dkey), 0, "e4m3")
    b = queryq.T @ dkeyq
    bm = b + f64(mask)
    s = np.concatenate([a, bm], axis=1)
    p = np.exp(s - np.max(s, axis=1, keepdims=True))
    w = p * f64(fac) / np.sum(p, axis=1, keepdims=True)
    wt = w.T
    valsq = mxq(f64(vals), 0, "e4m3")
    wtq = mxq(wt, 0, "e4m3")
    o = valsq.T @ wtq
    words, scales = planes(o)
    return o, words, scales

@@ -1,0 +1,229 @@
+from contextlib import ExitStack
+
+import concourse.mybir as mybir
+
+D, T, I, Q, E, J, C = 512, 2048, 512, 256, 512, 512, 1024
+FLOPS = 2 * D * Q * (I + J) + 2 * C * E * Q
+
+F32 = mybir.dt.float32
+BF16 = mybir.dt.bfloat16
+I32 = mybir.dt.int32
+U32 = mybir.dt.uint32
+U16 = mybir.dt.uint16
+U8 = mybir.dt.uint8
+FP8X4 = mybir.dt.float8_e4m3fn_x4
+FP4X4 = mybir.dt.float4_e2m1fn_x4
+ALU = mybir.AluOpType
+ACT = mybir.ActivationFunctionType
+
+P = 128
+PACK = 4
+PASS = P * PACK
+Q_TILES = Q // P
+C_PASSES = C // PASS
+V_ON_VECTOR = ((0, 1, 1), (1, 0, 1))
+DK_ON_VECTOR = (0, 16)
+V_ON_GPSIMD = ()
+
+
+def tile_attend_treeverify_pl_kernel(tc, query, keys_words, keys_scales, dkey, mask, fac, vals, offs, out_0, out_1, out_2):
+    nc = tc.nc
+    with ExitStack() as ctx:
+        sb = ctx.enter_context(tc.tile_pool(name="sb", bufs=1))
+        ps = ctx.enter_context(tc.psum_pool(name="ps", bufs=1))
+
+        def tile(name, shape, dtype):
+            return sb.tile(shape, dtype, name=name, align_bytes=64)
+
+        def bank(tag, name):
+            return ps.tile([P, 512], F32, name=name, tag=tag)
+
+        offsets = tile("offsets", [P, I // 16], U16)
+        key_words = tile("key_words", [P, T], U16)
+        key_scales = tile("key_scales", [P, T], U8)
+        q_raw = tile("q_raw", [P, PACK, Q], F32)
+        ident = tile("ident", [P, P], F32)
+        zeros = sb.tile([P, P], F32, name="zeros", tag="staging", align_bytes=64)
+        nc.gpsimd.memset(key_scales[:].bitcast(I32), 0)
+        nc.gpsimd.memset(zeros[:], 0.0)
+        nc.gpsimd.affine_select(out=ident[:], in_=zeros[:], compare_op=ALU.not_equal, fill=1.0, base=0, pattern=[[-1, P]], channel_multiplier=1)
+
+        nc.sync.dma_start(offsets[:], offs)
+        nc.sync.dma_start(key_words[:].bitcast(I32), keys_words[0].bitcast(I32))
+        for quad in range(4):
+            nc.scalar.dma_start(key_scales[32 * quad : 32 * quad + 4, :].bitcast(I32), keys_scales[0, 4 * quad : 4 * quad + 4, :].bitcast(I32))
+        nc.sync.dma_start(q_raw[:], query.rearrange("(p j) q -> p j q", j=PACK))
+
+        piece = PACK * 256
+        staging = sb.tile([P, 7 * piece + 16], F32, name="staging", tag="staging", align_bytes=64)
+
+        def rows_of(k):
+            return staging[:, k * piece : (k + 1) * piece].rearrange("p (j n) -> p j n", j=PACK)
+
+        dk_raw = [rows_of(h) for h in range(2)]
+        v_raw = [[rows_of(2 + 2 * g + h) for h in range(2)] for g in range(C_PASSES)]
+        mask_sb = [staging[:, 6 * piece + n * J : 6 * piece + (n + 1) * J] for n in range(Q_TILES)]
+        fac_cols = staging[:, 7 * piece : 7 * piece + 8].rearrange("p (g t) -> p g t", t=PACK)
+        dkey_rows = dkey.rearrange("(p j) (h n) -> h p j n", j=PACK, h=2)
+        vals_rows = vals.rearrange("(g p j) (h e) -> g h p j e", g=C_PASSES, j=PACK, h=2)
+        mask_rows = mask.rearrange("(n p) j -> n p j", p=P)
+        fac_rows = fac[0].rearrange("(g p t) -> p g t", g=C_PASSES, t=PACK)
+        nc.sync.dma_start(dk_raw[0], dkey_rows[0])
+        nc.sync.dma_start(dk_raw[1], dkey_rows[1])
+        nc.sync.dma_start(fac_cols, fac_rows)
+        nc.sync.dma_start(v_raw[0][0], vals_rows[0, 0])
+        nc.sync.dma_start(mask_sb[0], mask_rows[0])
+        nc.sync.dma_start(v_raw[0][1], vals_rows[0, 1])
+        nc.sync.dma_start(v_raw[1][0], vals_rows[1, 0])
+        nc.sync.dma_start(mask_sb[1], mask_rows[1])
+        nc.sync.dma_start(v_raw[1][1], vals_rows[1, 1])
+
+        keys_g = tile("keys_g", [P, I], U16)
+        key_scales_g = tile("key_scales_g", [P, I], U8)
+        nc.vector.tensor_copy(keys_g[:], key_words[:].indirect(offsets[:]))
+        nc.vector.tensor_copy(key_scales_g[:], key_scales[:].indirect(offsets[:]))
+
+        def quantize(codes, scales, grouped):
+            nc.vector.quantize_mx(out=codes.bitcast(FP8X4), scales=scales, in_=grouped)
+
+        def woven(grouped, raw):
+            return grouped.rearrange("p (c i t) -> p c t i", i=4, t=PACK), raw.rearrange("p t (c i) -> p c t i", i=4)
+
+        q_bf = tile("q_bf", [P, Q * PACK], BF16)
+        q_codes = tile("q_codes", [P, Q], U32)
+        q_scales = tile("q_scales", [P, Q], U8)
+        dst, src = woven(q_bf[:], q_raw[:])
+        nc.scalar.activation(dst, src, ACT.Copy, scale=-1.0)
+        quantize(q_codes[:], q_scales[:], q_bf[:])
+
+        dk_codes = tile("dk_codes", [P, J], U32)
+        dk_scales = tile("dk_scales", [P, J], U8)
+        for h in range(2):
+            dk_bf = tile("dk_bf%d" % h, [P, J * PACK // 2], BF16)
+            dst, src = woven(dk_bf[:], dk_raw[h])
+            cut = 64 - DK_ON_VECTOR[h]
+            if cut > 0:
+                nc.scalar.copy(dst[:, 0:cut], src[:, 0:cut])
+            if cut < 64:
+                nc.vector.tensor_copy(dst[:, cut:64], src[:, cut:64])
+            cols = slice(h * (J // 2), (h + 1) * (J // 2))
+            quantize(dk_codes[:, cols], dk_scales[:, cols], dk_bf[:])
+
+        a_ps = [bank("bank%d" % n, "a_ps%d" % n) for n in range(Q_TILES)]
+        b_ps = [bank("bank%d" % (2 + n), "b_ps%d" % n) for n in range(Q_TILES)]
+        for n in range(Q_TILES):
+            rows = slice(n * P, (n + 1) * P)
+            nc.tensor.matmul_mx(out=a_ps[n][:], lhsT=q_codes[:, rows].bitcast(FP8X4), lhsT_scale=q_scales[:, rows],
+                                rhs=keys_g[:].bitcast(FP4X4), rhs_scale=key_scales_g[:], start=True, stop=True)
+        for n in range(Q_TILES):
+            rows = slice(n * P, (n + 1) * P)
+            nc.tensor.matmul_mx(out=b_ps[n][:], lhsT=q_codes[:, rows].bitcast(FP8X4), lhsT_scale=q_scales[:, rows],
+                                rhs=dk_codes[:].bitcast(FP8X4), rhs_scale=dk_scales[:], start=True, stop=True)
+
+        fac_ps = [bank("bank%d" % (4 + g), "fac_ps%d" % g) for g in range(C_PASSES)]
+        for g in range(C_PASSES):
+            dealt = fac_ps[g][:].rearrange("q (u p e) -> q u e p", u=2, e=2)
+            for t in range(PACK):
+                nc.tensor.transpose(dealt[:, t // 2, t % 2, :], fac_cols[:, g, t : t + 1].to_broadcast([P, P]), ident[:])
+
+        def deal(ap):
+            return ap.rearrange("q (p u e) -> q u p e", u=2, e=2)
+
+        def as_dealt(ap):
+            return ap.rearrange("q (u p e) -> q u p e", u=2, e=2)
+
+        prob = [tile("prob%d" % n, [P, C], F32) for n in range(Q_TILES)]
+        total = [tile("total%d" % n, [P, 1], F32) for n in range(Q_TILES)]
+        w_codes = [[tile("w_codes%d%d" % (n, g), [P, P], U32) for g in range(C_PASSES)] for n in range(Q_TILES)]
+        w_scales = [[tile("w_scales%d%d" % (n, g), [P, P], U8) for g in range(C_PASSES)] for n in range(Q_TILES)]
+        v_codes = [tile("v_codes%d" % g, [P, E], U32) for g in range(C_PASSES)]
+        v_scales = [tile("v_scales%d" % g, [P, E], U8) for g in range(C_PASSES)]
+        o_codes = tile("o_codes", [P, Q], I32)
+        o_scales = tile("o_scales", [P, Q], U8)
+        out_rows = out_0.rearrange("(p t) q -> p t q", t=PACK)
+        out_words = out_1[0].rearrange("p q t -> p (q t)").bitcast(I32)
+
+        def exponentials(n):
+            neg_s = tile("neg_s%d" % n, [P, C], F32)
+            min_a = tile("min_a%d" % n, [P, 1], F32)
+            min_s = tile("min_s%d" % n, [P, 1], F32)
+            nc.vector.tensor_scalar(as_dealt(neg_s[:, 0:I]), deal(a_ps[n][:]), 1.0, None, ALU.mult, ALU.min, accum_out=min_a[:])
+            nc.vector.tensor_tensor(as_dealt(neg_s[:, I:C]), deal(b_ps[n][:]), deal(mask_sb[n]), ALU.subtract)
+            nc.vector.tensor_scalar(neg_s[:, I:C], neg_s[:, I:C], 1.0, min_a[:], ALU.mult, ALU.min, accum_out=min_s[:])
+            nc.scalar.activation(prob[n][:], neg_s[:], ACT.Exp, bias=min_s[:], scale=-1.0, accum_out=total[n][:])
+
+        def weights(n, banks):
+            inverse = tile("inverse%d" % n, [P, 1], F32)
+            nc.vector.reciprocal(inverse[:], total[n][:])
+            for g in range(C_PASSES):
+                w_bf = tile("w_bf%d%d" % (n, g), [P, PASS], BF16)
+                nc.vector.scalar_tensor_tensor(w_bf[:], prob[n][:, g * PASS : (g + 1) * PASS], inverse[:], fac_ps[g][:], ALU.mult, ALU.mult)
+                wt_ps = bank(banks[g], "wt_ps%d%d" % (n, g))
+                words = w_bf[:].bitcast(F32)
+                for u in range(2):
+                    nc.tensor.transpose(wt_ps[:, u * P : (u + 1) * P], words[:, u * P : (u + 1) * P], ident[:])
+                wt_bf = tile("wt_bf%d%d" % (n, g), [P, PASS], BF16)
+                nc.scalar.copy(wt_bf[:].bitcast(F32).rearrange("p (q u) -> p q u", u=2),
+                               wt_ps[:, 0 : 2 * P].rearrange("p (u q) -> p q u", u=2))
+                quantize(w_codes[n][g][:], w_scales[n][g][:], wt_bf[:])
+
+        def values(g):
+            v_bf = tile("v_bf%d" % g, [P, E * PACK], BF16)
+            dst = v_bf[:].rearrange("p (t h k m j) -> p h k m j t", t=PACK, j=PACK, h=2, k=2)
+            for h in range(2):
+                src = v_raw[g][h].rearrange("p j (k m t) -> p k m j t", t=PACK, k=2)
+                for k in range(2):
+                    if (g, h, k) in V_ON_VECTOR:
+                        nc.vector.tensor_copy(dst[:, h, k], src[:, k])
+                    elif (g, h, k) in V_ON_GPSIMD:
+                        nc.gpsimd.tensor_scalar(dst[:, h, k], src[:, k], 1.0, 0.0, ALU.mult, ALU.add)
+                    else:
+                        nc.scalar.copy(dst[:, h, k], src[:, k])
+            quantize(v_codes[g][:], v_scales[g][:], v_bf[:])
+
+        def product(out, n, t, g):
+            feat = slice(t * P, (t + 1) * P)
+            nc.tensor.matmul_mx(out=out, lhsT=v_codes[g][:, feat].bitcast(FP8X4), lhsT_scale=v_scales[g][:, feat],
+                                rhs=w_codes[n][g][:].bitcast(FP8X4), rhs_scale=w_scales[n][g][:],
+                                start=(g == 0), stop=(g == C_PASSES - 1))
+
+        def hand_out(n, o_sb, o_bf):
+            rows = slice(n * P, (n + 1) * P)
+            nc.sync.dma_start(out_rows[:, :, rows], o_sb[:])
+            quantize(o_codes[:, rows], o_scales[:, rows], o_bf[:])
+            nc.sync.dma_start(out_words[:, rows], o_codes[:, rows])
+
+        def output_one_bank(n, tag):
+            o_ps = bank(tag, "o_ps%d" % n)
+            for t in range(PACK):
+                for g in range(C_PASSES):
+                    product(o_ps[:, t * P : (t + 1) * P], n, t, g)
+            o_bf = tile("o_bf%d" % n, [P, P * PACK], BF16)
+            o_sb = tile("o_sb%d" % n, [P, PACK, P], F32)
+            nc.scalar.copy(o_sb[:].rearrange("p t q -> p (t q)"), o_ps[:])
+            nc.vector.tensor_copy(o_bf[:].rearrange("p (c i t) -> p c t i", i=4, t=PACK), o_sb[:].rearrange("p t (c i) -> p c t i", i=4))
+            hand_out(n, o_sb, o_bf)
+
+        def output_four_banks(n, tags):
+            o_ps = [bank(tags[t], "o_ps%d%d" % (n, t)) for t in range(PACK)]
+            o_bf = tile("o_bf%d" % n, [P, P * PACK], BF16)
+            o_sb = tile("o_sb%d" % n, [P, PACK, P], F32)
+            for g in range(C_PASSES):
+                for t in range(PACK):
+                    product(o_ps[t][:, 0:P], n, t, g)
+            for t in range(PACK):
+                nc.scalar.copy(o_sb[:, t, :], o_ps[t][:, 0:P])
+            nc.vector.tensor_copy(o_bf[:].rearrange("p (c i t) -> p c t i", i=4, t=PACK), o_sb[:].rearrange("p t (c i) -> p c t i", i=4))
+            hand_out(n, o_sb, o_bf)
+
+        exponentials(0)
+        exponentials(1)
+        weights(0, ("bank0", "bank2"))
+        weights(1, ("bank1", "bank3"))
+        values(0)
+        values(1)
+        output_one_bank(0, "bank6")
+        output_four_banks(1, ("bank7", "bank0", "bank2", "bank4"))
+        for quad in range(4):
+            queue = nc.sync if quad % 2 == 0 else nc.scalar
+            queue.dma_start(out_2[0, 4 * quad : 4 * quad + 4, :].bitcast(I32), o_scales[32 * quad : 32 * quad + 4, :].bitcast(I32))

@@ -21,9 +21,10 @@ PACK = 4
 PASS = P * PACK
 Q_TILES = Q // P
 C_PASSES = C // PASS
-V_ON_VECTOR = ((0, 1, 1), (1, 0, 1))
-DK_ON_VECTOR = (0, 16)
-V_ON_GPSIMD = ()
+VALS_ON_VECTOR = ((1, 1),)
+VALS_ON_GPSIMD = ()
+LATE_HALF = (1, 0)
+VALS_PIECE = 64
 
 
 def tile_attend_treeverify_pl_kernel(tc, query, keys_words, keys_scales, dkey, mask, fac, vals, offs, out_0, out_1, out_2):
@@ -35,8 +36,8 @@ def tile_attend_treeverify_pl_kernel(tc, query, keys_words, keys_scales, dkey, m
         def tile(name, shape, dtype):
             return sb.tile(shape, dtype, name=name, align_bytes=64)
 
-        def bank(tag, name):
-            return ps.tile([P, 512], F32, name=name, tag=tag)
+        def bank(number, name):
+            return ps.tile([P, 512], F32, name=name, tag="bank%d" % number)
 
         offsets = tile("offsets", [P, I // 16], U16)
         key_words = tile("key_words", [P, T], U16)
@@ -54,29 +55,26 @@ def tile_attend_treeverify_pl_kernel(tc, query, keys_words, keys_scales, dkey, m
             nc.scalar.dma_start(key_scales[32 * quad : 32 * quad + 4, :].bitcast(I32), keys_scales[0, 4 * quad : 4 * quad + 4, :].bitcast(I32))
         nc.sync.dma_start(q_raw[:], query.rearrange("(p j) q -> p j q", j=PACK))
 
-        piece = PACK * 256
-        staging = sb.tile([P, 7 * piece + 16], F32, name="staging", tag="staging", align_bytes=64)
+        piece = PACK * 512
+        staging = sb.tile([P, 3 * piece + 2 * J + 16], F32, name="staging", tag="staging", align_bytes=64)
 
         def rows_of(k):
             return staging[:, k * piece : (k + 1) * piece].rearrange("p (j n) -> p j n", j=PACK)
 
-        dk_raw = [rows_of(h) for h in range(2)]
-        v_raw = [[rows_of(2 + 2 * g + h) for h in range(2)] for g in range(C_PASSES)]
-        mask_sb = [staging[:, 6 * piece + n * J : 6 * piece + (n + 1) * J] for n in range(Q_TILES)]
-        fac_cols = staging[:, 7 * piece : 7 * piece + 8].rearrange("p (g t) -> p g t", t=PACK)
-        dkey_rows = dkey.rearrange("(p j) (h n) -> h p j n", j=PACK, h=2)
-        vals_rows = vals.rearrange("(g p j) (h e) -> g h p j e", g=C_PASSES, j=PACK, h=2)
+        dk_raw = rows_of(0)
+        v_raw = [rows_of(1 + g) for g in range(C_PASSES)]
+        mask_sb = [staging[:, 3 * piece + n * J : 3 * piece + (n + 1) * J] for n in range(Q_TILES)]
+        fac_cols = staging[:, 3 * piece + 2 * J : 3 * piece + 2 * J + 8].rearrange("p (g t) -> p g t", t=PACK)
+        dkey_rows = dkey.rearrange("(p j) n -> p j n", j=PACK)
+        vals_rows = vals.rearrange("(g p j) e -> g p j e", g=C_PASSES, j=PACK)
         mask_rows = mask.rearrange("(n p) j -> n p j", p=P)
         fac_rows = fac[0].rearrange("(g p t) -> p g t", g=C_PASSES, t=PACK)
-        nc.sync.dma_start(dk_raw[0], dkey_rows[0])
-        nc.sync.dma_start(dk_raw[1], dkey_rows[1])
-        nc.sync.dma_start(fac_cols, fac_rows)
-        nc.sync.dma_start(v_raw[0][0], vals_rows[0, 0])
+        nc.sync.dma_start(dk_raw, dkey_rows)
+        nc.sync.dma_start(v_raw[0], vals_rows[0])
         nc.sync.dma_start(mask_sb[0], mask_rows[0])
-        nc.sync.dma_start(v_raw[0][1], vals_rows[0, 1])
-        nc.sync.dma_start(v_raw[1][0], vals_rows[1, 0])
+        nc.sync.dma_start(fac_cols, fac_rows)
         nc.sync.dma_start(mask_sb[1], mask_rows[1])
-        nc.sync.dma_start(v_raw[1][1], vals_rows[1, 1])
+        nc.sync.dma_start(v_raw[1], vals_rows[1])
 
         keys_g = tile("keys_g", [P, I], U16)
         key_scales_g = tile("key_scales_g", [P, I], U8)
@@ -99,18 +97,17 @@ def tile_attend_treeverify_pl_kernel(tc, query, keys_words, keys_scales, dkey, m
         dk_codes = tile("dk_codes", [P, J], U32)
         dk_scales = tile("dk_scales", [P, J], U8)
         for h in range(2):
-            dk_bf = tile("dk_bf%d" % h, [P, J * PACK // 2], BF16)
-            dst, src = woven(dk_bf[:], dk_raw[h])
-            cut = 64 - DK_ON_VECTOR[h]
-            if cut > 0:
-                nc.scalar.copy(dst[:, 0:cut], src[:, 0:cut])
-            if cut < 64:
-                nc.vector.tensor_copy(dst[:, cut:64], src[:, cut:64])
             cols = slice(h * (J // 2), (h + 1) * (J // 2))
+            dk_bf = tile("dk_bf%d" % h, [P, J * PACK // 2], BF16)
+            dst, src = woven(dk_bf[:], dk_raw[:, :, cols])
+            if h == 0:
+                nc.scalar.copy(dst, src)
+            else:
+                nc.vector.tensor_copy(dst, src)
             quantize(dk_codes[:, cols], dk_scales[:, cols], dk_bf[:])
 
-        a_ps = [bank("bank%d" % n, "a_ps%d" % n) for n in range(Q_TILES)]
-        b_ps = [bank("bank%d" % (2 + n), "b_ps%d" % n) for n in range(Q_TILES)]
+        a_ps = [bank(n, "a_ps%d" % n) for n in range(Q_TILES)]
+        b_ps = [bank(2 + n, "b_ps%d" % n) for n in range(Q_TILES)]
         for n in range(Q_TILES):
             rows = slice(n * P, (n + 1) * P)
             nc.tensor.matmul_mx(out=a_ps[n][:], lhsT=q_codes[:, rows].bitcast(FP8X4), lhsT_scale=q_scales[:, rows],
@@ -120,18 +117,14 @@ def tile_attend_treeverify_pl_kernel(tc, query, keys_words, keys_scales, dkey, m
             nc.tensor.matmul_mx(out=b_ps[n][:], lhsT=q_codes[:, rows].bitcast(FP8X4), lhsT_scale=q_scales[:, rows],
                                 rhs=dk_codes[:].bitcast(FP8X4), rhs_scale=dk_scales[:], start=True, stop=True)
 
-        fac_ps = [bank("bank%d" % (4 + g), "fac_ps%d" % g) for g in range(C_PASSES)]
-        for g in range(C_PASSES):
-            dealt = fac_ps[g][:].rearrange("q (u p e) -> q u e p", u=2, e=2)
-            for t in range(PACK):
-                nc.tensor.transpose(dealt[:, t // 2, t % 2, :], fac_cols[:, g, t : t + 1].to_broadcast([P, P]), ident[:])
-
         def deal(ap):
             return ap.rearrange("q (p u e) -> q u p e", u=2, e=2)
 
         def as_dealt(ap):
             return ap.rearrange("q (u p e) -> q u p e", u=2, e=2)
 
+        neg_s = [sb.tile([P, C], F32, name="neg_s%d" % n, tag="scores%d" % n, align_bytes=64) for n in range(Q_TILES)]
+        min_s = [tile("min_s%d" % n, [P, 1], F32) for n in range(Q_TILES)]
         prob = [tile("prob%d" % n, [P, C], F32) for n in range(Q_TILES)]
         total = [tile("total%d" % n, [P, 1], F32) for n in range(Q_TILES)]
         w_codes = [[tile("w_codes%d%d" % (n, g), [P, P], U32) for g in range(C_PASSES)] for n in range(Q_TILES)]
@@ -143,43 +136,51 @@ def tile_attend_treeverify_pl_kernel(tc, query, keys_words, keys_scales, dkey, m
         out_rows = out_0.rearrange("(p t) q -> p t q", t=PACK)
         out_words = out_1[0].rearrange("p q t -> p (q t)").bitcast(I32)
 
-        def exponentials(n):
-            neg_s = tile("neg_s%d" % n, [P, C], F32)
+        for n in range(Q_TILES):
             min_a = tile("min_a%d" % n, [P, 1], F32)
-            min_s = tile("min_s%d" % n, [P, 1], F32)
-            nc.vector.tensor_scalar(as_dealt(neg_s[:, 0:I]), deal(a_ps[n][:]), 1.0, None, ALU.mult, ALU.min, accum_out=min_a[:])
-            nc.vector.tensor_tensor(as_dealt(neg_s[:, I:C]), deal(b_ps[n][:]), deal(mask_sb[n]), ALU.subtract)
-            nc.vector.tensor_scalar(neg_s[:, I:C], neg_s[:, I:C], 1.0, min_a[:], ALU.mult, ALU.min, accum_out=min_s[:])
-            nc.scalar.activation(prob[n][:], neg_s[:], ACT.Exp, bias=min_s[:], scale=-1.0, accum_out=total[n][:])
+            nc.vector.tensor_scalar(as_dealt(neg_s[n][:, 0:I]), deal(a_ps[n][:]), 1.0, None, ALU.mult, ALU.min, accum_out=min_a[:])
+            nc.vector.tensor_tensor(as_dealt(neg_s[n][:, I:C]), deal(b_ps[n][:]), deal(mask_sb[n]), ALU.subtract)
+            nc.vector.tensor_scalar(neg_s[n][:, I:C], neg_s[n][:, I:C], 1.0, min_a[:], ALU.mult, ALU.min, accum_out=min_s[n][:])
 
-        def weights(n, banks):
+        fac_ps = [bank(g, "fac_ps%d" % g) for g in range(C_PASSES)]
+        for g in range(C_PASSES):
+            dealt = fac_ps[g][:].rearrange("q (u p e) -> q u e p", u=2, e=2)
+            for t in range(PACK):
+                nc.tensor.transpose(dealt[:, t // 2, t % 2, :], fac_cols[:, g, t : t + 1].to_broadcast([P, P]), ident[:])
+
+        def exponentials(n):
+            nc.scalar.activation(prob[n][:], neg_s[n][:], ACT.Exp, bias=min_s[n][:], scale=-1.0, accum_out=total[n][:])
+
+        def weights(n):
             inverse = tile("inverse%d" % n, [P, 1], F32)
             nc.vector.reciprocal(inverse[:], total[n][:])
             for g in range(C_PASSES):
                 w_bf = tile("w_bf%d%d" % (n, g), [P, PASS], BF16)
                 nc.vector.scalar_tensor_tensor(w_bf[:], prob[n][:, g * PASS : (g + 1) * PASS], inverse[:], fac_ps[g][:], ALU.mult, ALU.mult)
-                wt_ps = bank(banks[g], "wt_ps%d%d" % (n, g))
+                wt_ps = bank(2 + g, "wt_ps%d%d" % (n, g))
                 words = w_bf[:].bitcast(F32)
                 for u in range(2):
                     nc.tensor.transpose(wt_ps[:, u * P : (u + 1) * P], words[:, u * P : (u + 1) * P], ident[:])
                 wt_bf = tile("wt_bf%d%d" % (n, g), [P, PASS], BF16)
-                nc.scalar.copy(wt_bf[:].bitcast(F32).rearrange("p (q u) -> p q u", u=2),
-                               wt_ps[:, 0 : 2 * P].rearrange("p (u q) -> p q u", u=2))
+                move = nc.vector.tensor_copy if (n, g) == (1, 1) else nc.scalar.copy
+                move(wt_bf[:].bitcast(F32).rearrange("p (q u) -> p q u", u=2), wt_ps[:, 0 : 2 * P].rearrange("p (u q) -> p q u", u=2))
                 quantize(w_codes[n][g][:], w_scales[n][g][:], wt_bf[:])
 
         def values(g):
-            v_bf = tile("v_bf%d" % g, [P, E * PACK], BF16)
-            dst = v_bf[:].rearrange("p (t h k m j) -> p h k m j t", t=PACK, j=PACK, h=2, k=2)
+            src = v_raw[g].rearrange("p j (m h t) -> p h m j t", h=2, t=2)
             for h in range(2):
-                src = v_raw[g][h].rearrange("p j (k m t) -> p k m j t", t=PACK, k=2)
-                for k in range(2):
-                    if (g, h, k) in V_ON_VECTOR:
-                        nc.vector.tensor_copy(dst[:, h, k], src[:, k])
-                    elif (g, h, k) in V_ON_GPSIMD:
-                        nc.gpsimd.tensor_scalar(dst[:, h, k], src[:, k], 1.0, 0.0, ALU.mult, ALU.add)
-                    else:
-                        nc.scalar.copy(dst[:, h, k], src[:, k])
-            quantize(v_codes[g][:], v_scales[g][:], v_bf[:])
+                tag = "scores0" if (g, h) == LATE_HALF else "v_bf%d%d" % (g, h)
+                v_bf = sb.tile([P, E * PACK // 2], BF16, name="v_bf%d%d" % (g, h), tag=tag, align_bytes=64)
+                dst = v_bf[:].rearrange("p (t m j) -> p m j t", t=2, j=PACK)
+                if (g, h) in VALS_ON_VECTOR:
+                    nc.vector.tensor_copy(dst, src[:, h])
+                elif (g, h) in VALS_ON_GPSIMD:
+                    nc.gpsimd.tensor_scalar(dst, src[:, h], 1.0, 0.0, ALU.mult, ALU.add)
+                else:
+                    for m in range(0, P, VALS_PIECE):
+                        nc.scalar.copy(dst[:, m : m + VALS_PIECE], src[:, h, m : m + VALS_PIECE])
+                cols = slice(h * (E // 2), (h + 1) * (E // 2))
+                quantize(v_codes[g][:, cols], v_scales[g][:, cols], v_bf[:])
 
         def product(out, n, t, g):
             feat = slice(t * P, (t + 1) * P)
@@ -187,43 +188,43 @@ def tile_attend_treeverify_pl_kernel(tc, query, keys_words, keys_scales, dkey, m
                                 rhs=w_codes[n][g][:].bitcast(FP8X4), rhs_scale=w_scales[n][g][:],
                                 start=(g == 0), stop=(g == C_PASSES - 1))
 
-        def hand_out(n, o_sb, o_bf):
+        def hand_out(n, o_sb):
             rows = slice(n * P, (n + 1) * P)
+            o_bf = tile("o_bf%d" % n, [P, P * PACK], BF16)
+            dst, src = woven(o_bf[:], o_sb[:])
+            nc.vector.tensor_copy(dst, src)
             nc.sync.dma_start(out_rows[:, :, rows], o_sb[:])
             quantize(o_codes[:, rows], o_scales[:, rows], o_bf[:])
             nc.sync.dma_start(out_words[:, rows], o_codes[:, rows])
 
-        def output_one_bank(n, tag):
-            o_ps = bank(tag, "o_ps%d" % n)
-            for t in range(PACK):
-                for g in range(C_PASSES):
-                    product(o_ps[:, t * P : (t + 1) * P], n, t, g)
-            o_bf = tile("o_bf%d" % n, [P, P * PACK], BF16)
+        def output_one_bank(n, numbers):
             o_sb = tile("o_sb%d" % n, [P, PACK, P], F32)
-            nc.scalar.copy(o_sb[:].rearrange("p t q -> p (t q)"), o_ps[:])
-            nc.vector.tensor_copy(o_bf[:].rearrange("p (c i t) -> p c t i", i=4, t=PACK), o_sb[:].rearrange("p t (c i) -> p c t i", i=4))
-            hand_out(n, o_sb, o_bf)
+            for h in range(2):
+                o_ps = bank(numbers[h], "o_ps%d%d" % (n, h))
+                for k in range(2):
+                    for g in range(C_PASSES):
+                        product(o_ps[:, k * P : (k + 1) * P], n, 2 * h + k, g)
+                nc.scalar.copy(o_sb[:, 2 * h : 2 * h + 2, :].rearrange("p t q -> p (t q)"), o_ps[:, 0 : 2 * P])
+            hand_out(n, o_sb)
 
-        def output_four_banks(n, tags):
-            o_ps = [bank(tags[t], "o_ps%d%d" % (n, t)) for t in range(PACK)]
-            o_bf = tile("o_bf%d" % n, [P, P * PACK], BF16)
+        def output_four_banks(n, numbers):
+            o_ps = [bank(numbers[t], "o_ps%d%d" % (n, t)) for t in range(PACK)]
             o_sb = tile("o_sb%d" % n, [P, PACK, P], F32)
             for g in range(C_PASSES):
                 for t in range(PACK):
                     product(o_ps[t][:, 0:P], n, t, g)
             for t in range(PACK):
                 nc.scalar.copy(o_sb[:, t, :], o_ps[t][:, 0:P])
-            nc.vector.tensor_copy(o_bf[:].rearrange("p (c i t) -> p c t i", i=4, t=PACK), o_sb[:].rearrange("p t (c i) -> p c t i", i=4))
-            hand_out(n, o_sb, o_bf)
+            hand_out(n, o_sb)
 
         exponentials(0)
         exponentials(1)
-        weights(0, ("bank0", "bank2"))
-        weights(1, ("bank1", "bank3"))
+        weights(0)
         values(0)
         values(1)
-        output_one_bank(0, "bank6")
-        output_four_banks(1, ("bank7", "bank0", "bank2", "bank4"))
+        weights(1)
+        output_one_bank(0, (4, 1))
+        output_four_banks(1, (5, 6, 7, 0))
         for quad in range(4):
             queue = nc.sync if quad % 2 == 0 else nc.scalar
             queue.dma_start(out_2[0, 4 * quad : 4 * quad + 4, :].bitcast(I32), o_scales[32 * quad : 32 * quad + 4, :].bitcast(I32))

@@ -21,10 +21,10 @@ PACK = 4
 PASS = P * PACK
 Q_TILES = Q // P
 C_PASSES = C // PASS
-VALS_ON_VECTOR = ((1, 1),)
-VALS_ON_GPSIMD = ()
+VALS_ON_VECTOR = ((1, 1, 1),)
+DKEY_ON_VECTOR = (0, 0)
+OUT_ON_VECTOR = ()
 LATE_HALF = (1, 0)
-VALS_PIECE = 64
 
 
 def tile_attend_treeverify_pl_kernel(tc, query, keys_words, keys_scales, dkey, mask, fac, vals, offs, out_0, out_1, out_2):
@@ -55,26 +55,29 @@ def tile_attend_treeverify_pl_kernel(tc, query, keys_words, keys_scales, dkey, m
             nc.scalar.dma_start(key_scales[32 * quad : 32 * quad + 4, :].bitcast(I32), keys_scales[0, 4 * quad : 4 * quad + 4, :].bitcast(I32))
         nc.sync.dma_start(q_raw[:], query.rearrange("(p j) q -> p j q", j=PACK))
 
-        piece = PACK * 512
-        staging = sb.tile([P, 3 * piece + 2 * J + 16], F32, name="staging", tag="staging", align_bytes=64)
+        piece = PACK * 256
+        staging = sb.tile([P, 7 * piece + 16], F32, name="staging", tag="staging", align_bytes=64)
 
         def rows_of(k):
             return staging[:, k * piece : (k + 1) * piece].rearrange("p (j n) -> p j n", j=PACK)
 
-        dk_raw = rows_of(0)
-        v_raw = [rows_of(1 + g) for g in range(C_PASSES)]
-        mask_sb = [staging[:, 3 * piece + n * J : 3 * piece + (n + 1) * J] for n in range(Q_TILES)]
-        fac_cols = staging[:, 3 * piece + 2 * J : 3 * piece + 2 * J + 8].rearrange("p (g t) -> p g t", t=PACK)
-        dkey_rows = dkey.rearrange("(p j) n -> p j n", j=PACK)
-        vals_rows = vals.rearrange("(g p j) e -> g p j e", g=C_PASSES, j=PACK)
+        dk_raw = [rows_of(h) for h in range(2)]
+        v_raw = [[rows_of(2 + 2 * g + h) for h in range(2)] for g in range(C_PASSES)]
+        mask_sb = [staging[:, 6 * piece + n * J : 6 * piece + (n + 1) * J] for n in range(Q_TILES)]
+        fac_cols = staging[:, 7 * piece : 7 * piece + 8].rearrange("p (g t) -> p g t", t=PACK)
+        dkey_rows = dkey.rearrange("(p j) (h n) -> h p j n", j=PACK, h=2)
+        vals_rows = vals.rearrange("(g p j) (h e) -> g h p j e", g=C_PASSES, j=PACK, h=2)
         mask_rows = mask.rearrange("(n p) j -> n p j", p=P)
         fac_rows = fac[0].rearrange("(g p t) -> p g t", g=C_PASSES, t=PACK)
-        nc.sync.dma_start(dk_raw, dkey_rows)
-        nc.sync.dma_start(v_raw[0], vals_rows[0])
+        nc.sync.dma_start(dk_raw[0], dkey_rows[0])
+        nc.sync.dma_start(dk_raw[1], dkey_rows[1])
+        nc.sync.dma_start(v_raw[0][0], vals_rows[0, 0])
         nc.sync.dma_start(mask_sb[0], mask_rows[0])
         nc.sync.dma_start(fac_cols, fac_rows)
+        nc.sync.dma_start(v_raw[0][1], vals_rows[0, 1])
         nc.sync.dma_start(mask_sb[1], mask_rows[1])
-        nc.sync.dma_start(v_raw[1], vals_rows[1])
+        nc.sync.dma_start(v_raw[1][0], vals_rows[1, 0])
+        nc.sync.dma_start(v_raw[1][1], vals_rows[1, 1])
 
         keys_g = tile("keys_g", [P, I], U16)
         key_scales_g = tile("key_scales_g", [P, I], U8)
@@ -98,12 +101,12 @@ def tile_attend_treeverify_pl_kernel(tc, query, keys_words, keys_scales, dkey, m
         dk_scales = tile("dk_scales", [P, J], U8)
         for h in range(2):
             cols = slice(h * (J // 2), (h + 1) * (J // 2))
-            dk_bf = tile("dk_bf%d" % h, [P, J * PACK // 2], BF16)
-            dst, src = woven(dk_bf[:], dk_raw[:, :, cols])
-            if h == 0:
-                nc.scalar.copy(dst, src)
-            else:
-                nc.vector.tensor_copy(dst, src)
+            dk_bf = sb.tile([P, J * PACK // 2], BF16, name="dk_bf%d" % h, tag=("dk_bf0", "scores1")[h], align_bytes=64)
+            dst, src = woven(dk_bf[:], dk_raw[h])
+            cut = 64 - DKEY_ON_VECTOR[h]
+            nc.scalar.copy(dst[:, 0:cut], src[:, 0:cut])
+            if cut < 64:
+                nc.vector.tensor_copy(dst[:, cut:64], src[:, cut:64])
             quantize(dk_codes[:, cols], dk_scales[:, cols], dk_bf[:])
 
         a_ps = [bank(n, "a_ps%d" % n) for n in range(Q_TILES)]
@@ -127,8 +130,8 @@ def tile_attend_treeverify_pl_kernel(tc, query, keys_words, keys_scales, dkey, m
         min_s = [tile("min_s%d" % n, [P, 1], F32) for n in range(Q_TILES)]
         prob = [tile("prob%d" % n, [P, C], F32) for n in range(Q_TILES)]
         total = [tile("total%d" % n, [P, 1], F32) for n in range(Q_TILES)]
-        w_codes = [[tile("w_codes%d%d" % (n, g), [P, P], U32) for g in range(C_PASSES)] for n in range(Q_TILES)]
-        w_scales = [[tile("w_scales%d%d" % (n, g), [P, P], U8) for g in range(C_PASSES)] for n in range(Q_TILES)]
+        w_codes = [tile("w_codes%d" % n, [P, C_PASSES * P], U32) for n in range(Q_TILES)]
+        w_scales = [tile("w_scales%d" % n, [P, C_PASSES * P], U8) for n in range(Q_TILES)]
         v_codes = [tile("v_codes%d" % g, [P, E], U32) for g in range(C_PASSES)]
         v_scales = [tile("v_scales%d" % g, [P, E], U8) for g in range(C_PASSES)]
         o_codes = tile("o_codes", [P, Q], I32)
@@ -151,41 +154,42 @@ def tile_attend_treeverify_pl_kernel(tc, query, keys_words, keys_scales, dkey, m
         def exponentials(n):
             nc.scalar.activation(prob[n][:], neg_s[n][:], ACT.Exp, bias=min_s[n][:], scale=-1.0, accum_out=total[n][:])
 
-        def weights(n):
+        def weights(n, groups):
             inverse = tile("inverse%d" % n, [P, 1], F32)
             nc.vector.reciprocal(inverse[:], total[n][:])
-            for g in range(C_PASSES):
-                w_bf = tile("w_bf%d%d" % (n, g), [P, PASS], BF16)
-                nc.vector.scalar_tensor_tensor(w_bf[:], prob[n][:, g * PASS : (g + 1) * PASS], inverse[:], fac_ps[g][:], ALU.mult, ALU.mult)
-                wt_ps = bank(2 + g, "wt_ps%d%d" % (n, g))
-                words = w_bf[:].bitcast(F32)
-                for u in range(2):
-                    nc.tensor.transpose(wt_ps[:, u * P : (u + 1) * P], words[:, u * P : (u + 1) * P], ident[:])
-                wt_bf = tile("wt_bf%d%d" % (n, g), [P, PASS], BF16)
-                move = nc.vector.tensor_copy if (n, g) == (1, 1) else nc.scalar.copy
-                move(wt_bf[:].bitcast(F32).rearrange("p (q u) -> p q u", u=2), wt_ps[:, 0 : 2 * P].rearrange("p (u q) -> p q u", u=2))
-                quantize(w_codes[n][g][:], w_scales[n][g][:], wt_bf[:])
+            for k, group in enumerate(groups):
+                wt_ps = bank(2 + n + k if len(groups) == 1 else 3 - k, "wt_ps%d%d" % (n, k))
+                for g in group:
+                    w_bf = tile("w_bf%d%d" % (n, g), [P, PASS], BF16)
+                    nc.vector.scalar_tensor_tensor(w_bf[:], prob[n][:, g * PASS : (g + 1) * PASS], inverse[:], fac_ps[g][:], ALU.mult, ALU.mult)
+                    words = w_bf[:].bitcast(F32)
+                    for u in range(2):
+                        place = 2 * (g - group[0]) + u
+                        nc.tensor.transpose(wt_ps[:, place * P : (place + 1) * P], words[:, u * P : (u + 1) * P], ident[:])
+                wt_bf = tile("wt_bf%d%d" % (n, k), [P, PASS * len(group)], BF16)
+                nc.scalar.copy(wt_bf[:].bitcast(F32).rearrange("p (g q u) -> p g q u", g=len(group), u=2),
+                               wt_ps[:, 0 : 2 * P * len(group)].rearrange("p (g u q) -> p g q u", g=len(group), u=2))
+                cols = slice(group[0] * P, (group[-1] + 1) * P)
+                quantize(w_codes[n][:, cols], w_scales[n][:, cols], wt_bf[:])
 
-        def values(g):
-            src = v_raw[g].rearrange("p j (m h t) -> p h m j t", h=2, t=2)
-            for h in range(2):
-                tag = "scores0" if (g, h) == LATE_HALF else "v_bf%d%d" % (g, h)
-                v_bf = sb.tile([P, E * PACK // 2], BF16, name="v_bf%d%d" % (g, h), tag=tag, align_bytes=64)
-                dst = v_bf[:].rearrange("p (t m j) -> p m j t", t=2, j=PACK)
-                if (g, h) in VALS_ON_VECTOR:
-                    nc.vector.tensor_copy(dst, src[:, h])
-                elif (g, h) in VALS_ON_GPSIMD:
-                    nc.gpsimd.tensor_scalar(dst, src[:, h], 1.0, 0.0, ALU.mult, ALU.add)
-                else:
-                    for m in range(0, P, VALS_PIECE):
-                        nc.scalar.copy(dst[:, m : m + VALS_PIECE], src[:, h, m : m + VALS_PIECE])
-                cols = slice(h * (E // 2), (h + 1) * (E // 2))
+        def values(g, tiles):
+            pairs = 2 // tiles
+            for k in range(tiles):
+                tag = "scores0" if (g, k) == LATE_HALF else "v_bf%d%d" % (g, k)
+                v_bf = sb.tile([P, E * PACK // tiles], BF16, name="v_bf%d%d" % (g, k), tag=tag, align_bytes=64)
+                dst = v_bf[:].rearrange("p (pair t h m j) -> p pair h m j t", pair=pairs, t=2, h=2, j=PACK)
+                for h in range(2):
+                    src = v_raw[g][h].rearrange("p j (m pair t) -> p pair m j t", pair=2, t=2)
+                    for pair in range(pairs):
+                        move = nc.vector.tensor_copy if (g, k, h) in VALS_ON_VECTOR else nc.scalar.copy
+                        move(dst[:, pair, h], src[:, k * pairs + pair])
+                cols = slice(k * (E // tiles), (k + 1) * (E // tiles))
                 quantize(v_codes[g][:, cols], v_scales[g][:, cols], v_bf[:])
 
         def product(out, n, t, g):
             feat = slice(t * P, (t + 1) * P)
             nc.tensor.matmul_mx(out=out, lhsT=v_codes[g][:, feat].bitcast(FP8X4), lhsT_scale=v_scales[g][:, feat],
-                                rhs=w_codes[n][g][:].bitcast(FP8X4), rhs_scale=w_scales[n][g][:],
+                                rhs=w_codes[n][:, g * P : (g + 1) * P].bitcast(FP8X4), rhs_scale=w_scales[n][:, g * P : (g + 1) * P],
                                 start=(g == 0), stop=(g == C_PASSES - 1))
 
         def hand_out(n, o_sb):
@@ -197,34 +201,33 @@ def tile_attend_treeverify_pl_kernel(tc, query, keys_words, keys_scales, dkey, m
             quantize(o_codes[:, rows], o_scales[:, rows], o_bf[:])
             nc.sync.dma_start(out_words[:, rows], o_codes[:, rows])
 
-        def output_one_bank(n, numbers):
-            o_sb = tile("o_sb%d" % n, [P, PACK, P], F32)
-            for h in range(2):
-                o_ps = bank(numbers[h], "o_ps%d%d" % (n, h))
-                for k in range(2):
-                    for g in range(C_PASSES):
-                        product(o_ps[:, k * P : (k + 1) * P], n, 2 * h + k, g)
-                nc.scalar.copy(o_sb[:, 2 * h : 2 * h + 2, :].rearrange("p t q -> p (t q)"), o_ps[:, 0 : 2 * P])
-            hand_out(n, o_sb)
+        o_ps = {}
 
-        def output_four_banks(n, numbers):
-            o_ps = [bank(numbers[t], "o_ps%d%d" % (n, t)) for t in range(PACK)]
-            o_sb = tile("o_sb%d" % n, [P, PACK, P], F32)
-            for g in range(C_PASSES):
-                for t in range(PACK):
-                    product(o_ps[t][:, 0:P], n, t, g)
+        def products(n, g, numbers=None):
             for t in range(PACK):
-                nc.scalar.copy(o_sb[:, t, :], o_ps[t][:, 0:P])
+                if g == 0:
+                    o_ps.setdefault((n, t), bank(numbers[t], "o_ps%d%d" % (n, t)))
+                product(o_ps[(n, t)][:, 0:P], n, t, g)
+
+        def output(n):
+            o_sb = tile("o_sb%d" % n, [P, PACK, P], F32)
+            for t in range(PACK):
+                move = nc.vector.tensor_copy if (n, t) in OUT_ON_VECTOR else nc.scalar.copy
+                move(o_sb[:, t, :], o_ps[(n, t)][:, 0:P])
             hand_out(n, o_sb)
 
         exponentials(0)
         exponentials(1)
-        weights(0)
-        values(0)
-        values(1)
-        weights(1)
-        output_one_bank(0, (4, 1))
-        output_four_banks(1, (5, 6, 7, 0))
+        weights(0, ((0, 1),))
+        values(0, 1)
+        values(1, 2)
+        weights(1, ((0,), (1,)))
+        products(0, 0, (4, 5, 6, 7))
+        products(0, 1)
+        products(1, 0, (0, 3, 1, 2))
+        products(1, 1)
+        output(0)
+        output(1)
         for quad in range(4):
             queue = nc.sync if quad % 2 == 0 else nc.scalar
             queue.dma_start(out_2[0, 4 * quad : 4 * quad + 4, :].bitcast(I32), o_scales[32 * quad : 32 * quad + 4, :].bitcast(I32))

@@ -158,7 +158,7 @@ def tile_attend_treeverify_pl_kernel(tc, query, keys_words, keys_scales, dkey, m
             inverse = tile("inverse%d" % n, [P, 1], F32)
             nc.vector.reciprocal(inverse[:], total[n][:])
             for k, group in enumerate(groups):
-                wt_ps = bank(2 + n + k if len(groups) == 1 else 3 - k, "wt_ps%d%d" % (n, k))
+                wt_ps = bank(2 + k, "wt_ps%d%d" % (n, k))
                 for g in group:
                     w_bf = tile("w_bf%d%d" % (n, g), [P, PASS], BF16)
                     nc.vector.scalar_tensor_tensor(w_bf[:], prob[n][:, g * PASS : (g + 1) * PASS], inverse[:], fac_ps[g][:], ALU.mult, ALU.mult)
@@ -218,13 +218,13 @@ def tile_attend_treeverify_pl_kernel(tc, query, keys_words, keys_scales, dkey, m
 
         exponentials(0)
         exponentials(1)
-        weights(0, ((0, 1),))
+        weights(0, ((0,), (1,)))
         values(0, 1)
         values(1, 2)
         weights(1, ((0,), (1,)))
         products(0, 0, (4, 5, 6, 7))
         products(0, 1)
-        products(1, 0, (0, 3, 1, 2))
+        products(1, 0, (0, 2, 1, 3))
         products(1, 1)
         output(0)
         output(1)

from contextlib import ExitStack

import concourse.mybir as mybir

D, T, I, Q, E, J, C = 512, 2048, 512, 256, 512, 512, 1024
FLOPS = 2 * D * Q * (I + J) + 2 * C * E * Q

F32 = mybir.dt.float32
BF16 = mybir.dt.bfloat16
I32 = mybir.dt.int32
U32 = mybir.dt.uint32
U16 = mybir.dt.uint16
U8 = mybir.dt.uint8
FP8X4 = mybir.dt.float8_e4m3fn_x4
FP4X4 = mybir.dt.float4_e2m1fn_x4
ALU = mybir.AluOpType
ACT = mybir.ActivationFunctionType

P = 128
PACK = 4
PASS = P * PACK
Q_TILES = Q // P
C_PASSES = C // PASS
VALS_ON_VECTOR = ((1, 1, 1),)
DKEY_ON_VECTOR = (0, 0)
OUT_ON_VECTOR = ()
LATE_HALF = (1, 0)


def tile_attend_treeverify_pl_kernel(tc, query, keys_words, keys_scales, dkey, mask, fac, vals, offs, out_0, out_1, out_2):
    nc = tc.nc
    with ExitStack() as ctx:
        sb = ctx.enter_context(tc.tile_pool(name="sb", bufs=1))
        ps = ctx.enter_context(tc.psum_pool(name="ps", bufs=1))

        def tile(name, shape, dtype):
            return sb.tile(shape, dtype, name=name, align_bytes=64)

        def bank(number, name):
            return ps.tile([P, 512], F32, name=name, tag="bank%d" % number)

        offsets = tile("offsets", [P, I // 16], U16)
        key_words = tile("key_words", [P, T], U16)
        key_scales = tile("key_scales", [P, T], U8)
        q_raw = tile("q_raw", [P, PACK, Q], F32)
        ident = tile("ident", [P, P], F32)
        zeros = sb.tile([P, P], F32, name="zeros", tag="staging", align_bytes=64)
        nc.gpsimd.memset(key_scales[:].bitcast(I32), 0)
        nc.gpsimd.memset(zeros[:], 0.0)
        nc.gpsimd.affine_select(out=ident[:], in_=zeros[:], compare_op=ALU.not_equal, fill=1.0, base=0, pattern=[[-1, P]], channel_multiplier=1)

        nc.sync.dma_start(offsets[:], offs)
        nc.sync.dma_start(key_words[:].bitcast(I32), keys_words[0].bitcast(I32))
        for quad in range(4):
            nc.scalar.dma_start(key_scales[32 * quad : 32 * quad + 4, :].bitcast(I32), keys_scales[0, 4 * quad : 4 * quad + 4, :].bitcast(I32))
        nc.sync.dma_start(q_raw[:], query.rearrange("(p j) q -> p j q", j=PACK))

        piece = PACK * 256
        staging = sb.tile([P, 7 * piece + 16], F32, name="staging", tag="staging", align_bytes=64)

        def rows_of(k):
            return staging[:, k * piece : (k + 1) * piece].rearrange("p (j n) -> p j n", j=PACK)

        dk_raw = [rows_of(h) for h in range(2)]
        v_raw = [[rows_of(2 + 2 * g + h) for h in range(2)] for g in range(C_PASSES)]
        mask_sb = [staging[:, 6 * piece + n * J : 6 * piece + (n + 1) * J] for n in range(Q_TILES)]
        fac_cols = staging[:, 7 * piece : 7 * piece + 8].rearrange("p (g t) -> p g t", t=PACK)
        dkey_rows = dkey.rearrange("(p j) (h n) -> h p j n", j=PACK, h=2)
        vals_rows = vals.rearrange("(g p j) (h e) -> g h p j e", g=C_PASSES, j=PACK, h=2)
        mask_rows = mask.rearrange("(n p) j -> n p j", p=P)
        fac_rows = fac[0].rearrange("(g p t) -> p g t", g=C_PASSES, t=PACK)
        nc.sync.dma_start(dk_raw[0], dkey_rows[0])
        nc.sync.dma_start(dk_raw[1], dkey_rows[1])
        nc.sync.dma_start(v_raw[0][0], vals_rows[0, 0])
        nc.sync.dma_start(mask_sb[0], mask_rows[0])
        nc.sync.dma_start(fac_cols, fac_rows)
        nc.sync.dma_start(v_raw[0][1], vals_rows[0, 1])
        nc.sync.dma_start(mask_sb[1], mask_rows[1])
        nc.sync.dma_start(v_raw[1][0], vals_rows[1, 0])
        nc.sync.dma_start(v_raw[1][1], vals_rows[1, 1])

        keys_g = tile("keys_g", [P, I], U16)
        key_scales_g = tile("key_scales_g", [P, I], U8)
        nc.vector.tensor_copy(keys_g[:], key_words[:].indirect(offsets[:]))
        nc.vector.tensor_copy(key_scales_g[:], key_scales[:].indirect(offsets[:]))

        def quantize(codes, scales, grouped):
            nc.vector.quantize_mx(out=codes.bitcast(FP8X4), scales=scales, in_=grouped)

        def woven(grouped, raw):
            return grouped.rearrange("p (c i t) -> p c t i", i=4, t=PACK), raw.rearrange("p t (c i) -> p c t i", i=4)

        q_bf = tile("q_bf", [P, Q * PACK], BF16)
        q_codes = tile("q_codes", [P, Q], U32)
        q_scales = tile("q_scales", [P, Q], U8)
        dst, src = woven(q_bf[:], q_raw[:])
        nc.scalar.activation(dst, src, ACT.Copy, scale=-1.0)
        quantize(q_codes[:], q_scales[:], q_bf[:])

        dk_codes = tile("dk_codes", [P, J], U32)
        dk_scales = tile("dk_scales", [P, J], U8)
        for h in range(2):
            cols = slice(h * (J // 2), (h + 1) * (J // 2))
            dk_bf = sb.tile([P, J * PACK // 2], BF16, name="dk_bf%d" % h, tag=("dk_bf0", "scores1")[h], align_bytes=64)
            dst, src = woven(dk_bf[:], dk_raw[h])
            cut = 64 - DKEY_ON_VECTOR[h]
            nc.scalar.copy(dst[:, 0:cut], src[:, 0:cut])
            if cut < 64:
                nc.vector.tensor_copy(dst[:, cut:64], src[:, cut:64])
            quantize(dk_codes[:, cols], dk_scales[:, cols], dk_bf[:])

        a_ps = [bank(n, "a_ps%d" % n) for n in range(Q_TILES)]
        b_ps = [bank(2 + n, "b_ps%d" % n) for n in range(Q_TILES)]
        for n in range(Q_TILES):
            rows = slice(n * P, (n + 1) * P)
            nc.tensor.matmul_mx(out=a_ps[n][:], lhsT=q_codes[:, rows].bitcast(FP8X4), lhsT_scale=q_scales[:, rows],
                                rhs=keys_g[:].bitcast(FP4X4), rhs_scale=key_scales_g[:], start=True, stop=True)
        for n in range(Q_TILES):
            rows = slice(n * P, (n + 1) * P)
            nc.tensor.matmul_mx(out=b_ps[n][:], lhsT=q_codes[:, rows].bitcast(FP8X4), lhsT_scale=q_scales[:, rows],
                                rhs=dk_codes[:].bitcast(FP8X4), rhs_scale=dk_scales[:], start=True, stop=True)

        def deal(ap):
            return ap.rearrange("q (p u e) -> q u p e", u=2, e=2)

        def as_dealt(ap):
            return ap.rearrange("q (u p e) -> q u p e", u=2, e=2)

        neg_s = [sb.tile([P, C], F32, name="neg_s%d" % n, tag="scores%d" % n, align_bytes=64) for n in range(Q_TILES)]
        min_s = [tile("min_s%d" % n, [P, 1], F32) for n in range(Q_TILES)]
        prob = [tile("prob%d" % n, [P, C], F32) for n in range(Q_TILES)]
        total = [tile("total%d" % n, [P, 1], F32) for n in range(Q_TILES)]
        w_codes = [tile("w_codes%d" % n, [P, C_PASSES * P], U32) for n in range(Q_TILES)]
        w_scales = [tile("w_scales%d" % n, [P, C_PASSES * P], U8) for n in range(Q_TILES)]
        v_codes = [tile("v_codes%d" % g, [P, E], U32) for g in range(C_PASSES)]
        v_scales = [tile("v_scales%d" % g, [P, E], U8) for g in range(C_PASSES)]
        o_codes = tile("o_codes", [P, Q], I32)
        o_scales = tile("o_scales", [P, Q], U8)
        out_rows = out_0.rearrange("(p t) q -> p t q", t=PACK)
        out_words = out_1[0].rearrange("p q t -> p (q t)").bitcast(I32)

        for n in range(Q_TILES):
            min_a = tile("min_a%d" % n, [P, 1], F32)
            nc.vector.tensor_scalar(as_dealt(neg_s[n][:, 0:I]), deal(a_ps[n][:]), 1.0, None, ALU.mult, ALU.min, accum_out=min_a[:])
            nc.vector.tensor_tensor(as_dealt(neg_s[n][:, I:C]), deal(b_ps[n][:]), deal(mask_sb[n]), ALU.subtract)
            nc.vector.tensor_scalar(neg_s[n][:, I:C], neg_s[n][:, I:C], 1.0, min_a[:], ALU.mult, ALU.min, accum_out=min_s[n][:])

        fac_ps = [bank(g, "fac_ps%d" % g) for g in range(C_PASSES)]
        for g in range(C_PASSES):
            dealt = fac_ps[g][:].rearrange("q (u p e) -> q u e p", u=2, e=2)
            for t in range(PACK):
                nc.tensor.transpose(dealt[:, t // 2, t % 2, :], fac_cols[:, g, t : t + 1].to_broadcast([P, P]), ident[:])

        def exponentials(n):
            nc.scalar.activation(prob[n][:], neg_s[n][:], ACT.Exp, bias=min_s[n][:], scale=-1.0, accum_out=total[n][:])

        def weights(n, groups):
            inverse = tile("inverse%d" % n, [P, 1], F32)
            nc.vector.reciprocal(inverse[:], total[n][:])
            for k, group in enumerate(groups):
                wt_ps = bank(2 + k, "wt_ps%d%d" % (n, k))
                for g in group:
                    w_bf = tile("w_bf%d%d" % (n, g), [P, PASS], BF16)
                    nc.vector.scalar_tensor_tensor(w_bf[:], prob[n][:, g * PASS : (g + 1) * PASS], inverse[:], fac_ps[g][:], ALU.mult, ALU.mult)
                    words = w_bf[:].bitcast(F32)
                    for u in range(2):
                        place = 2 * (g - group[0]) + u
                        nc.tensor.transpose(wt_ps[:, place * P : (place + 1) * P], words[:, u * P : (u + 1) * P], ident[:])
                wt_bf = tile("wt_bf%d%d" % (n, k), [P, PASS * len(group)], BF16)
                nc.scalar.copy(wt_bf[:].bitcast(F32).rearrange("p (g q u) -> p g q u", g=len(group), u=2),
                               wt_ps[:, 0 : 2 * P * len(group)].rearrange("p (g u q) -> p g q u", g=len(group), u=2))
                cols = slice(group[0] * P, (group[-1] + 1) * P)
                quantize(w_codes[n][:, cols], w_scales[n][:, cols], wt_bf[:])

        def values(g, tiles):
            pairs = 2 // tiles
            for k in range(tiles):
                tag = "scores0" if (g, k) == LATE_HALF else "v_bf%d%d" % (g, k)
                v_bf = sb.tile([P, E * PACK // tiles], BF16, name="v_bf%d%d" % (g, k), tag=tag, align_bytes=64)
                dst = v_bf[:].rearrange("p (pair t h m j) -> p pair h m j t", pair=pairs, t=2, h=2, j=PACK)
                for h in range(2):
                    src = v_raw[g][h].rearrange("p j (m pair t) -> p pair m j t", pair=2, t=2)
                    for pair in range(pairs):
                        move = nc.vector.tensor_copy if (g, k, h) in VALS_ON_VECTOR else nc.scalar.copy
                        move(dst[:, pair, h], src[:, k * pairs + pair])
                cols = slice(k * (E // tiles), (k + 1) * (E // tiles))
                quantize(v_codes[g][:, cols], v_scales[g][:, cols], v_bf[:])

        def product(out, n, t, g):
            feat = slice(t * P, (t + 1) * P)
            nc.tensor.matmul_mx(out=out, lhsT=v_codes[g][:, feat].bitcast(FP8X4), lhsT_scale=v_scales[g][:, feat],
                                rhs=w_codes[n][:, g * P : (g + 1) * P].bitcast(FP8X4), rhs_scale=w_scales[n][:, g * P : (g + 1) * P],
                                start=(g == 0), stop=(g == C_PASSES - 1))

        def hand_out(n, o_sb):
            rows = slice(n * P, (n + 1) * P)
            o_bf = tile("o_bf%d" % n, [P, P * PACK], BF16)
            dst, src = woven(o_bf[:], o_sb[:])
            nc.vector.tensor_copy(dst, src)
            nc.sync.dma_start(out_rows[:, :, rows], o_sb[:])
            quantize(o_codes[:, rows], o_scales[:, rows], o_bf[:])
            nc.sync.dma_start(out_words[:, rows], o_codes[:, rows])

        o_ps = {}

        def products(n, g, numbers=None):
            for t in range(PACK):
                if g == 0:
                    o_ps.setdefault((n, t), bank(numbers[t], "o_ps%d%d" % (n, t)))
                product(o_ps[(n, t)][:, 0:P], n, t, g)

        def output(n):
            o_sb = tile("o_sb%d" % n, [P, PACK, P], F32)
            for t in range(PACK):
                move = nc.vector.tensor_copy if (n, t) in OUT_ON_VECTOR else nc.scalar.copy
                move(o_sb[:, t, :], o_ps[(n, t)][:, 0:P])
            hand_out(n, o_sb)

        exponentials(0)
        exponentials(1)
        weights(0, ((0,), (1,)))
        values(0, 1)
        values(1, 2)
        weights(1, ((0,), (1,)))
        products(0, 0, (4, 5, 6, 7))
        products(0, 1)
        products(1, 0, (0, 2, 1, 3))
        products(1, 1)
        output(0)
        output(1)
        for quad in range(4):
            queue = nc.sync if quad % 2 == 0 else nc.scalar
            queue.dma_start(out_2[0, 4 * quad : 4 * quad + 4, :].bitcast(I32), o_scales[32 * quad : 32 * quad + 4, :].bitcast(I32))
